import numpy as np
import ml_dtypes


def mxq(x, axis, fmt="e4m3"):
    dtype, down = {"e4m3": (ml_dtypes.float8_e4m3fn, 7), "e5m2": (ml_dtypes.float8_e5m2, 14)}[fmt]
    v = np.moveaxis(np.asarray(x, np.float32).astype(ml_dtypes.bfloat16).astype(np.float64), axis, -1)
    blocks = v.reshape(v.shape[:-1] + (-1, 32))
    amax = np.abs(blocks).max(-1, keepdims=True)
    byte = np.maximum(np.where(amax > 0, np.frexp(amax)[1] - 1 + 127, 0) - down, 1)
    scale = np.exp2(byte - 127.0)
    codes = (blocks / scale).astype(np.float32).astype(dtype).astype(np.float64)
    return np.moveaxis((codes * scale).reshape(v.shape), -1, axis)


WIDE = False


def mx_kscale(k):
    if not WIDE:
        return np.ones(k)
    levels = np.array([10, -10, 5, -5, 0])
    if k % 512:
        return np.exp2(np.random.permutation(np.resize(levels, k // 32))).repeat(32)
    a = np.empty((k // 512, 16))
    for p in range(k // 512):
        a[p, :8] = np.random.permutation(np.resize(levels, 8))
        for g in range(8):
            far = levels[np.abs(levels - a[p, g]) >= 10]
            a[p, g + 8] = far[np.random.randint(len(far))]
    return np.exp2(a.ravel()).repeat(32)


def f64(x):
    return np.asarray(x).astype(np.float64)


def striped(idx):
    return np.tile(idx.reshape(-1, 16).T, (8, 1)).astype(np.uint16)


def unstriped(offs):
    return offs[:16].T.reshape(-1).astype(np.int64)


def striped8(idx):
    return np.concatenate([x.reshape(-1, 16).T for x in idx]).astype(np.uint16)


def runs(offs, k):
    lists = np.stack([offs[16 * r : 16 * r + 16].T.reshape(-1) for r in range(8)]).astype(np.int64)
    return lists[np.arange(k) % 512 // 64]


def pack_weight(w):
    k, n = w.shape
    w = f64(np.asarray(w, np.float32).astype(ml_dtypes.bfloat16)).reshape(k // 32, 32, n)
    amax = np.abs(w).max(1)
    byte = np.clip(np.where(amax > 0, np.frexp(amax)[1] - 1 + 127 - 7, 1), 1, 254)
    scaled = (w * np.exp2(127.0 - byte)[:, None, :]).reshape(k, n).astype(np.float32)
    words = np.ascontiguousarray(scaled.reshape(k // 512, 128, 4, n).transpose(0, 1, 3, 2)).astype(ml_dtypes.float8_e4m3fn).view(np.uint8)
    return words, np.ascontiguousarray(byte.astype(np.uint8).reshape(k // 512, 16, n))


def unpack_weight(words, scales):
    g, p, n, _ = words.shape
    vals = np.ascontiguousarray(words).view(ml_dtypes.float8_e4m3fn).astype(np.float64) * np.repeat(np.exp2(scales.astype(np.float64) - 127.0), 8, axis=1)[..., None]
    return vals.transpose(0, 1, 3, 2).reshape(g * 512, n)


def sigmoid(v):
    return 1.0 / (1.0 + np.exp(-np.maximum(v, -700.0)))

def planes(y):
    n, m = y.shape
    v = y.astype(np.float32).astype(ml_dtypes.bfloat16).astype(np.float64).reshape(n // 32, 32, m)
    top = np.abs(v).max(1)
    byte = np.clip(np.where(top > 0, np.frexp(top)[1] - 1 + 127 - 7, 1), 1, 254)
    codes = (v * np.exp2(127.0 - byte)[:, None, :]).reshape(n, m).astype(np.float32).astype(ml_dtypes.float8_e4m3fn).view(np.uint8)
    words = codes.reshape(n // 512, 128, 4, m).transpose(0, 1, 3, 2)
    return np.ascontiguousarray(words), np.ascontiguousarray(byte.astype(np.uint8).reshape(n // 512, 16, m))


K, T, S, N, H, W = 512, 2048, 512, 512, 512, 256


def setup_inputs():
    n = np.random.standard_normal
    s = mx_kscale(K)[:, None]
    u = mx_kscale(H)
    packed_xT = pack_weight(n((K, T)) * s)
    packed_w1 = pack_weight(n((K, H)) / np.sqrt(K) / s)
    packed_w2 = pack_weight(n((H, N)) / np.sqrt(H) / u[:, None])
    perm = np.stack([np.random.permutation(S) for _ in range(8)])
    return {
        "x_words": packed_xT[0],
        "x_scales": packed_xT[1],
        "w1_words": packed_w1[0],
        "w1_scales": packed_w1[1],
        "gn": (np.random.uniform(0.5, 1.5, (H, 1)) * u[:, None]).astype(np.float32),
        "w2_words": packed_w2[0],
        "w2_scales": packed_w2[1],
        "offs": striped(np.random.permutation(T)[:S]),
        "n1": striped8(np.stack([np.random.permutation(S) for _ in range(8)])),
        "n2": striped8(perm[:, :W]),
        "n3": striped8(perm[:, W:]),
    }


def reference(x_words, x_scales, w1_words, w1_scales, gn, w2_words, w2_scales, offs, n1, n2, n3):
    xq = unpack_weight(x_words, x_scales)[:, unstriped(offs)]
    y = unpack_weight(w1_words, w1_scales).T @ xq
    st = y - (y[np.arange(H)[:, None], runs(n1, H)])
    z = f64(gn) * (st - (0.5 * (st[np.arange(H)[:, None], runs(n1, H)])))
    h = unpack_weight(w2_words, w2_scales).T @ mxq(z, 0, "e4m3")
    pa = h[np.arange(N)[:, None], runs(n2, N)]
    pb = h[np.arange(N)[:, None], runs(n3, N)]
    ra = pa * sigmoid(pb)
    out = h.copy()
    out[np.arange(N)[:, None], runs(n3, N)] = ra
    return (out,) + planes(out)

@@ -1,0 +1,209 @@
+from contextlib import ExitStack
+
+import concourse.mybir as mybir
+
+K, T, S, N, H, W = 512, 2048, 512, 512, 512, 256
+FLOPS = 2 * K * H * S + 2 * H * N * S
+
+F32 = mybir.dt.float32
+BF16 = mybir.dt.bfloat16
+I32 = mybir.dt.int32
+U32 = mybir.dt.uint32
+U16 = mybir.dt.uint16
+U8 = mybir.dt.uint8
+FP8X4 = mybir.dt.float8_e4m3fn_x4
+ALU = mybir.AluOpType
+ACT = mybir.ActivationFunctionType
+
+P = 128
+PACK = 4
+HALF = S // 2
+W1_ROW = 0
+W2_ROW = 0
+CHUNKS = ((0, 256), (256, 128), (384, 128))
+V_COLS = 256
+
+
+def tile_picked_laytwicefold_none_po_kernel(
+    tc, x_words, x_scales, w1_words, w1_scales, gn, w2_words, w2_scales, offs, n1, n2, n3, out_0, out_1, out_2
+):
+    nc = tc.nc
+    with ExitStack() as ctx:
+        keep = ctx.enter_context(tc.tile_pool(name="keep", bufs=1))
+        psum = ctx.enter_context(tc.psum_pool(name="psum", bufs=8))
+
+        def sb(name, shape, dtype, tag=None):
+            return keep.tile(shape, dtype, name=name, tag=tag or name, align_bytes=64)
+
+        def words_of(dram):
+            return dram[0].rearrange("p n r -> p (n r)").bitcast(I32)
+
+        def load_scale_rows(queue, plane, dram):
+            width = dram.shape[2] // 4
+            for q in range(4):
+                queue.dma_start(
+                    out=plane[32 * q : 32 * q + 32, :].bitcast(I32),
+                    in_=dram[0, 4 * q : 4 * q + 4, :].bitcast(I32).unsqueeze(0).to_broadcast([8, 4, width]),
+                )
+
+        offs_t = keep.tile([P, S // 16], U16, name="offs_t")
+        n1_t = keep.tile([P, S // 16], U16, name="n1_t")
+        n2_t = keep.tile([P, W // 16], U16, name="n2_t")
+        n3_t = keep.tile([P, W // 16], U16, name="n3_t")
+        xw = sb("xw", [P, T], I32)
+        xs = sb("xs", [P, T], U8)
+        w1w_raw = sb("w1w_raw", [P, H], I32)
+        w1s_raw = sb("w1s_raw", [P, H], U8)
+        w2w_raw = sb("w2w_raw", [P, N], I32)
+        w2s_raw = sb("w2s_raw", [P, N], U8)
+        gn_t = sb("gn_t", [P, PACK], F32)
+
+        load_scale_rows(nc.sync, xs, x_scales)
+        nc.sync.dma_start(offs_t[:], offs)
+        nc.sync.dma_start(out=xw[:], in_=words_of(x_words))
+        nc.sync.dma_start(out=w1w_raw[:], in_=words_of(w1_words))
+        load_scale_rows(nc.sync, w1s_raw, w1_scales)
+        nc.sync.dma_start(n1_t[:], n1)
+        nc.sync.dma_start(out=w2w_raw[:], in_=words_of(w2_words))
+        load_scale_rows(nc.sync, w2s_raw, w2_scales)
+        nc.sync.dma_start(n2_t[:], n2)
+        nc.sync.dma_start(n3_t[:], n3)
+        nc.gpsimd.dma_start(out=gn_t[:], in_=gn.rearrange("(p t) o -> p (t o)", t=PACK))
+        warm = sb("warm", [P, 2], F32)
+        nc.gpsimd.memset(warm[:, 0:1], 0.0)
+        nc.scalar.activation(warm[:, 1:2], warm[:, 0:1], ACT.Sigmoid)
+
+        def deal(name, raw, dtype, tag=None):
+            dealt = sb(name, [P, PACK * P], dtype, tag)
+            nc.vector.tensor_copy(
+                out=dealt[:].rearrange("p (t m) -> p t m", t=PACK), in_=raw[:].rearrange("p (m t) -> p t m", t=PACK)
+            )
+            return dealt
+
+        w1w = deal("w1w", w1w_raw, I32)
+        xs_g = sb("xs_g", [P, S], U8)
+        nc.vector.tensor_copy(xs_g[:], xs[:].indirect(offs_t[:]))
+        w1s = deal("w1s", w1s_raw, U8)
+        gn_half = sb("gn_half", [P, PACK], F32)
+        nc.scalar.activation(gn_half[:], gn_t[:], ACT.Copy, scale=0.5)
+
+        y_ps = {}
+        for u in range(2):
+            xw_g = sb("xw_g%d" % u, [P, HALF], U32)
+            nc.vector.tensor_copy(xw_g[:], xw[:].bitcast(U32).indirect(offs_t[:, 16 * u : 16 * (u + 1)]))
+            for t in range(PACK):
+                if u == 0 or t == 0:
+                    y_ps[t, u] = psum.tile([P, S], F32, name="acc", tag="acc")
+                else:
+                    y_ps[t, u] = y_ps[t, 0]
+                nc.tensor.matmul_mx(
+                    out=y_ps[t, u][:, u * HALF : (u + 1) * HALF],
+                    lhsT=w1w[:, t * P : (t + 1) * P].bitcast(FP8X4),
+                    lhsT_scale=w1s[W1_ROW:P, t * P : (t + 1) * P],
+                    rhs=xw_g[:].bitcast(FP8X4),
+                    rhs_scale=xs_g[:, u * HALF : (u + 1) * HALF],
+                    start=True,
+                    stop=True,
+                )
+
+
+        ya = [sb("ya%d" % t, [P, S], F32) for t in range(PACK)]
+        yb = [sb("yb%d" % t, [P, S], F32) for t in range(PACK)]
+        sc = [sb("sc%d" % t, [P, S], F32) for t in range(PACK)]
+        sh = [sb("sh%d" % t, [P, S], F32) for t in range(PACK)]
+
+        def evict(dst, t, u, cols):
+            nc.scalar.activation(dst[t][:, cols], y_ps[t, u][:, cols], ACT.Copy, scale=gn_half[:, t : t + 1])
+
+        for t in range(PACK):
+            if t == 0:
+                for u in range(2):
+                    evict(ya, t, u, slice(u * HALF, (u + 1) * HALF))
+                    evict(yb, t, u, slice(u * HALF, (u + 1) * HALF))
+            else:
+                evict(ya, t, 0, slice(0, S))
+                evict(yb, t, 0, slice(0, S))
+            for u in range(2):
+                cols = slice(u * HALF, (u + 1) * HALF)
+                nc.vector.tensor_tensor(
+                    sc[t][:, cols], ya[t][:].indirect(n1_t[:, 16 * u : 16 * (u + 1)]), yb[t][:, cols], ALU.subtract
+                )
+        w2w = deal("w2w", w2w_raw, I32, "yb0")
+        w2s = deal("w2s", w2s_raw, U8, "yb1")
+        for t in range(PACK):
+            nc.scalar.activation(sh[t][:], sc[t][:], ACT.Copy, scale=-2.0)
+
+        ht = [sb("ht%d" % t, [P, S], F32) for t in range(PACK)]
+        zb = {}
+
+        def gather_z(c):
+            c0, w = CHUNKS[c]
+            zf = sb("zf%d" % c, [P, PACK, w], F32, tag="zb0" if c == 2 else None)
+            for t in range(PACK):
+                nc.vector.tensor_tensor(
+                    zf[:, t, :], sc[t][:].indirect(n1_t[:, c0 // 16 : (c0 + w) // 16]), sh[t][:, c0 : c0 + w], ALU.add
+                )
+            zb[c] = sb("zb%d" % c, [P, PACK * w], BF16)
+            dst = zb[c][:].rearrange("p (c i t) -> p c t i", i=4, t=PACK)
+            src = zf[:].rearrange("p t (c i) -> p c t i", i=4)
+            if c == len(CHUNKS) - 1:
+                nc.vector.tensor_copy(out=dst, in_=src)
+            else:
+                nc.scalar.copy(out=dst, in_=src)
+
+        def second_layer(c):
+            c0, w = CHUNKS[c]
+            zw = sb("zw%d" % c, [P, w], U32)
+            zs = sb("zs%d" % c, [P, w], U8)
+            nc.vector.quantize_mx(out=zw[:].bitcast(FP8X4), scales=zs[:], in_=zb[c][:])
+            for t in range(PACK):
+                acc = psum.tile([P, S], F32, name="acc", tag="acc")
+                nc.tensor.matmul_mx(
+                    out=acc[:, :w],
+                    lhsT=w2w[:, t * P : (t + 1) * P].bitcast(FP8X4),
+                    lhsT_scale=w2s[W2_ROW:P, t * P : (t + 1) * P],
+                    rhs=zw[:].bitcast(FP8X4),
+                    rhs_scale=zs[:],
+                    start=True,
+                    stop=True,
+                )
+                if (c, t) == (2, 0):
+                    nc.vector.tensor_copy(ht[t][:, c0 : c0 + w], acc[:, :w])
+                else:
+                    nc.scalar.copy(ht[t][:, c0 : c0 + w], acc[:, :w])
+
+        gather_z(0)
+        gather_z(1)
+        second_layer(0)
+        gather_z(2)
+        second_layer(1)
+        second_layer(2)
+
+        out_rows = out_0.rearrange("(p t) n -> t p n", t=PACK)
+        ob = sb("ob", [P, S, PACK], BF16)
+        for t in range(PACK):
+            pa = sb("pa%d" % t, [P, W], F32)
+            sg = sb("sg%d" % t, [P, W], F32)
+            nc.scalar.activation(sg[:], ht[t][:].indirect(n3_t[:]), ACT.Sigmoid)
+            nc.vector.tensor_copy(pa[:], ht[t][:].indirect(n2_t[:]))
+            nc.vector.tensor_tensor(ht[t][:].indirect(n3_t[:]), pa[:], sg[:], ALU.mult)
+            nc.sync.dma_start(out=out_rows[t], in_=ht[t][:])
+            if t < 2:
+                nc.scalar.copy(ob[:, :, t], ht[t][:])
+            else:
+                nc.vector.tensor_copy(ob[:, :V_COLS, t], ht[t][:, :V_COLS])
+                nc.scalar.copy(ob[:, V_COLS:, t], ht[t][:, V_COLS:])
+
+        ow = sb("ow", [P, S], I32)
+        osc = sb("osc", [P, S], U8)
+        out_words = words_of(out_1)
+        for u in range(2):
+            cols = slice(u * HALF, (u + 1) * HALF)
+            nc.vector.quantize_mx(
+                out=ow[:, cols].bitcast(FP8X4), scales=osc[:, cols], in_=ob[:, cols, :].rearrange("p n t -> p (n t)")
+            )
+            nc.sync.dma_start(out=out_words[:, cols], in_=ow[:, cols])
+        for q in range(4):
+            nc.scalar.dma_start(
+                out=out_2[0, 4 * q : 4 * q + 4, :].bitcast(I32), in_=osc[32 * q : 32 * q + 4, :].bitcast(I32)
+            )

@@ -76,22 +76,27 @@ def tile_picked_laytwicefold_none_po_kernel(
         def deal(name, raw, dtype, tag=None):
             dealt = sb(name, [P, PACK * P], dtype, tag)
             nc.vector.tensor_copy(
-                out=dealt[:].rearrange("p (t m) -> p t m", t=PACK), in_=raw[:].rearrange("p (m t) -> p t m", t=PACK)
+                out=dealt[:].rearrange("p (t m) -> p m t", t=PACK), in_=raw[:].rearrange("p (m t) -> p m t", t=PACK)
             )
             return dealt
 
-        w1w = deal("w1w", w1w_raw, I32)
         xs_g = sb("xs_g", [P, S], U8)
         nc.vector.tensor_copy(xs_g[:], xs[:].indirect(offs_t[:]))
-        w1s = deal("w1s", w1s_raw, U8)
         gn_half = sb("gn_half", [P, PACK], F32)
         nc.scalar.activation(gn_half[:], gn_t[:], ACT.Copy, scale=0.5)
 
         y_ps = {}
-        for u in range(2):
-            xw_g = sb("xw_g%d" % u, [P, HALF], U32)
-            nc.vector.tensor_copy(xw_g[:], xw[:].bitcast(U32).indirect(offs_t[:, 16 * u : 16 * (u + 1)]))
-            for t in range(PACK):
+        xw_g = [sb("xw_g%d" % u, [P, HALF], U32) for u in range(2)]
+
+        def gather_words(u):
+            nc.vector.tensor_copy(xw_g[u][:], xw[:].bitcast(U32).indirect(offs_t[:, 16 * u : 16 * (u + 1)]))
+
+        gather_words(0)
+        w1w = deal("w1w", w1w_raw, I32)
+        w1s = deal("w1s", w1s_raw, U8)
+        gather_words(1)
+        for t in range(PACK):
+            for u in range(2):
                 if u == 0 or t == 0:
                     y_ps[t, u] = psum.tile([P, S], F32, name="acc", tag="acc")
                 else:
@@ -100,12 +105,13 @@ def tile_picked_laytwicefold_none_po_kernel(
                     out=y_ps[t, u][:, u * HALF : (u + 1) * HALF],
                     lhsT=w1w[:, t * P : (t + 1) * P].bitcast(FP8X4),
                     lhsT_scale=w1s[W1_ROW:P, t * P : (t + 1) * P],
-                    rhs=xw_g[:].bitcast(FP8X4),
+                    rhs=xw_g[u][:].bitcast(FP8X4),
                     rhs_scale=xs_g[:, u * HALF : (u + 1) * HALF],
                     start=True,
                     stop=True,
                 )
 
+        w2w = deal("w2w", w2w_raw, I32)
 
         ya = [sb("ya%d" % t, [P, S], F32) for t in range(PACK)]
         yb = [sb("yb%d" % t, [P, S], F32) for t in range(PACK)]
@@ -128,24 +134,28 @@ def tile_picked_laytwicefold_none_po_kernel(
                 nc.vector.tensor_tensor(
                     sc[t][:, cols], ya[t][:].indirect(n1_t[:, 16 * u : 16 * (u + 1)]), yb[t][:, cols], ALU.subtract
                 )
-        w2w = deal("w2w", w2w_raw, I32, "yb0")
-        w2s = deal("w2s", w2s_raw, U8, "yb1")
+        w2s = deal("w2s", w2s_raw, U8, "yb0")
         for t in range(PACK):
             nc.scalar.activation(sh[t][:], sc[t][:], ACT.Copy, scale=-2.0)
 
         ht = [sb("ht%d" % t, [P, S], F32) for t in range(PACK)]
-        zb = {}
+        shared = sb("shared", [P, 768], F32)
+        zb = [shared[:, 0:512].bitcast(BF16), shared[:, 512:768].bitcast(BF16), sb("zb2", [P, 512], BF16)[:]]
+        zfs = [sb("zf0", [P, 1024], F32)[:], sb("zf1", [P, 512], F32)[:], shared[:, 256:768]]
 
-        def gather_z(c):
+        def gather_z(c, tiles):
             c0, w = CHUNKS[c]
-            zf = sb("zf%d" % c, [P, PACK, w], F32, tag="zb0" if c == 2 else None)
-            for t in range(PACK):
+            for t in tiles:
                 nc.vector.tensor_tensor(
-                    zf[:, t, :], sc[t][:].indirect(n1_t[:, c0 // 16 : (c0 + w) // 16]), sh[t][:, c0 : c0 + w], ALU.add
+                    zfs[c][:, t * w : (t + 1) * w],
+                    sc[t][:].indirect(n1_t[:, c0 // 16 : (c0 + w) // 16]),
+                    sh[t][:, c0 : c0 + w],
+                    ALU.add,
                 )
-            zb[c] = sb("zb%d" % c, [P, PACK * w], BF16)
-            dst = zb[c][:].rearrange("p (c i t) -> p c t i", i=4, t=PACK)
-            src = zf[:].rearrange("p t (c i) -> p c t i", i=4)
+
+        def weave(c):
+            dst = zb[c].rearrange("p (c i t) -> p c t i", i=4, t=PACK)
+            src = zfs[c].rearrange("p (t c i) -> p c t i", i=4, t=PACK)
             if c == len(CHUNKS) - 1:
                 nc.vector.tensor_copy(out=dst, in_=src)
             else:
@@ -155,7 +165,7 @@ def tile_picked_laytwicefold_none_po_kernel(
             c0, w = CHUNKS[c]
             zw = sb("zw%d" % c, [P, w], U32)
             zs = sb("zs%d" % c, [P, w], U8)
-            nc.vector.quantize_mx(out=zw[:].bitcast(FP8X4), scales=zs[:], in_=zb[c][:])
+            nc.vector.quantize_mx(out=zw[:].bitcast(FP8X4), scales=zs[:], in_=zb[c])
             for t in range(PACK):
                 acc = psum.tile([P, S], F32, name="acc", tag="acc")
                 nc.tensor.matmul_mx(
@@ -167,32 +177,38 @@ def tile_picked_laytwicefold_none_po_kernel(
                     start=True,
                     stop=True,
                 )
-                if (c, t) == (2, 0):
-                    nc.vector.tensor_copy(ht[t][:, c0 : c0 + w], acc[:, :w])
-                else:
-                    nc.scalar.copy(ht[t][:, c0 : c0 + w], acc[:, :w])
+                nc.scalar.copy(ht[t][:, c0 : c0 + w], acc[:, :w])
 
-        gather_z(0)
-        gather_z(1)
+        gather_z(0, range(PACK))
+        weave(0)
+        gather_z(1, range(PACK))
+        weave(1)
         second_layer(0)
-        gather_z(2)
+        gather_z(2, (0, 1))
         second_layer(1)
+        gather_z(2, (2, 3))
+        weave(2)
         second_layer(2)
 
         out_rows = out_0.rearrange("(p t) n -> t p n", t=PACK)
         ob = sb("ob", [P, S, PACK], BF16)
+        pa = [sb("pa%d" % t, [P, W], F32) for t in range(PACK)]
+        sg = [sb("sg%d" % t, [P, W], F32) for t in range(PACK)]
         for t in range(PACK):
-            pa = sb("pa%d" % t, [P, W], F32)
-            sg = sb("sg%d" % t, [P, W], F32)
-            nc.scalar.activation(sg[:], ht[t][:].indirect(n3_t[:]), ACT.Sigmoid)
-            nc.vector.tensor_copy(pa[:], ht[t][:].indirect(n2_t[:]))
-            nc.vector.tensor_tensor(ht[t][:].indirect(n3_t[:]), pa[:], sg[:], ALU.mult)
+            nc.scalar.activation(sg[t][:], ht[t][:].indirect(n3_t[:]), ACT.Sigmoid)
+        nc.vector.tensor_copy(pa[0][:], ht[0][:].indirect(n2_t[:]))
+        for t in range(PACK):
+            if t + 1 < PACK:
+                nc.vector.tensor_copy(pa[t + 1][:], ht[t + 1][:].indirect(n2_t[:]))
+            if t == 3:
+                nc.vector.tensor_copy(ob[:, :V_COLS, 2], ht[2][:, :V_COLS])
+            nc.vector.tensor_tensor(ht[t][:].indirect(n3_t[:]), pa[t][:], sg[t][:], ALU.mult)
             nc.sync.dma_start(out=out_rows[t], in_=ht[t][:])
             if t < 2:
                 nc.scalar.copy(ob[:, :, t], ht[t][:])
             else:
-                nc.vector.tensor_copy(ob[:, :V_COLS, t], ht[t][:, :V_COLS])
                 nc.scalar.copy(ob[:, V_COLS:, t], ht[t][:, V_COLS:])
+        nc.vector.tensor_copy(ob[:, :V_COLS, 3], ht[3][:, :V_COLS])
 
         ow = sb("ow", [P, S], I32)
         osc = sb("osc", [P, S], U8)

@@ -17,11 +17,12 @@ ACT = mybir.ActivationFunctionType
 
 P = 128
 PACK = 4
+QUADRANT = 32
+LIST_COL = 16
+LINE = 4
 HALF = S // 2
-W1_ROW = 0
-W2_ROW = 0
+PSUM_BANKS = 8
 CHUNKS = ((0, 256), (256, 128), (384, 128))
-V_COLS = 256
 
 
 def tile_picked_laytwicefold_none_po_kernel(
@@ -30,7 +31,7 @@ def tile_picked_laytwicefold_none_po_kernel(
     nc = tc.nc
     with ExitStack() as ctx:
         keep = ctx.enter_context(tc.tile_pool(name="keep", bufs=1))
-        psum = ctx.enter_context(tc.psum_pool(name="psum", bufs=8))
+        psum = ctx.enter_context(tc.psum_pool(name="psum", bufs=PSUM_BANKS))
 
         def sb(name, shape, dtype, tag=None):
             return keep.tile(shape, dtype, name=name, tag=tag or name, align_bytes=64)
@@ -38,18 +39,19 @@ def tile_picked_laytwicefold_none_po_kernel(
         def words_of(dram):
             return dram[0].rearrange("p n r -> p (n r)").bitcast(I32)
 
-        def load_scale_rows(queue, plane, dram):
-            width = dram.shape[2] // 4
-            for q in range(4):
-                queue.dma_start(
-                    out=plane[32 * q : 32 * q + 32, :].bitcast(I32),
-                    in_=dram[0, 4 * q : 4 * q + 4, :].bitcast(I32).unsqueeze(0).to_broadcast([8, 4, width]),
-                )
+        def entries(list_tile, start, count):
+            return list_tile[:, start // LIST_COL : (start + count) // LIST_COL]
 
-        offs_t = keep.tile([P, S // 16], U16, name="offs_t")
-        n1_t = keep.tile([P, S // 16], U16, name="n1_t")
-        n2_t = keep.tile([P, W // 16], U16, name="n2_t")
-        n3_t = keep.tile([P, W // 16], U16, name="n3_t")
+        def scale_rows(dram, q):
+            return dram[0, PACK * q : PACK * (q + 1), :].bitcast(I32)
+
+        def live_rows(tile, q):
+            return tile[QUADRANT * q : QUADRANT * q + PACK, :].bitcast(I32)
+
+        offs_t = keep.tile([P, S // LIST_COL], U16, name="offs_t")
+        n1_t = keep.tile([P, S // LIST_COL], U16, name="n1_t")
+        n2_t = keep.tile([P, W // LIST_COL], U16, name="n2_t")
+        n3_t = keep.tile([P, W // LIST_COL], U16, name="n3_t")
         xw = sb("xw", [P, T], I32)
         xs = sb("xs", [P, T], U8)
         w1w_raw = sb("w1w_raw", [P, H], I32)
@@ -58,168 +60,176 @@ def tile_picked_laytwicefold_none_po_kernel(
         w2s_raw = sb("w2s_raw", [P, N], U8)
         gn_t = sb("gn_t", [P, PACK], F32)
 
-        load_scale_rows(nc.sync, xs, x_scales)
+        nc.vector.memset(w1s_raw[:].bitcast(I32), 0)
+        nc.vector.memset(w2s_raw[:].bitcast(I32), 0)
+        for q in range(P // QUADRANT):
+            nc.sync.dma_start(
+                out=xs[QUADRANT * q : QUADRANT * (q + 1), :].bitcast(I32),
+                in_=scale_rows(x_scales, q).unsqueeze(0).to_broadcast([QUADRANT // PACK, PACK, T // 4]),
+            )
         nc.sync.dma_start(offs_t[:], offs)
         nc.sync.dma_start(out=xw[:], in_=words_of(x_words))
         nc.sync.dma_start(out=w1w_raw[:], in_=words_of(w1_words))
-        load_scale_rows(nc.sync, w1s_raw, w1_scales)
+        for q in range(P // QUADRANT):
+            nc.sync.dma_start(out=live_rows(w1s_raw, q), in_=scale_rows(w1_scales, q))
         nc.sync.dma_start(n1_t[:], n1)
         nc.sync.dma_start(out=w2w_raw[:], in_=words_of(w2_words))
-        load_scale_rows(nc.sync, w2s_raw, w2_scales)
+        for q in range(P // QUADRANT):
+            nc.sync.dma_start(out=live_rows(w2s_raw, q), in_=scale_rows(w2_scales, q))
         nc.sync.dma_start(n2_t[:], n2)
         nc.sync.dma_start(n3_t[:], n3)
         nc.gpsimd.dma_start(out=gn_t[:], in_=gn.rearrange("(p t) o -> p (t o)", t=PACK))
-        warm = sb("warm", [P, 2], F32)
-        nc.gpsimd.memset(warm[:, 0:1], 0.0)
-        nc.scalar.activation(warm[:, 1:2], warm[:, 0:1], ACT.Sigmoid)
 
-        def deal(name, raw, dtype, tag=None):
-            dealt = sb(name, [P, PACK * P], dtype, tag)
+        half = sb("half", [P, 2], F32)
+        nc.gpsimd.memset(half[:, 0:1], 0.0)
+        nc.scalar.activation(half[:, 1:2], half[:, 0:1], ACT.Sigmoid)
+
+        def deal(dealt, raw, t0, t1):
             nc.vector.tensor_copy(
-                out=dealt[:].rearrange("p (t m) -> p m t", t=PACK), in_=raw[:].rearrange("p (m t) -> p m t", t=PACK)
+                out=dealt[:].rearrange("p (t m) -> p m t", t=PACK)[:, :, t0:t1],
+                in_=raw[:].rearrange("p (m t) -> p m t", t=PACK)[:, :, t0:t1],
             )
-            return dealt
 
-        xs_g = sb("xs_g", [P, S], U8)
-        nc.vector.tensor_copy(xs_g[:], xs[:].indirect(offs_t[:]))
+        xs_picked = sb("xs_picked", [P, S], U8)
+        nc.vector.tensor_copy(xs_picked[:], xs[:].indirect(offs_t[:]))
         gn_half = sb("gn_half", [P, PACK], F32)
-        nc.scalar.activation(gn_half[:], gn_t[:], ACT.Copy, scale=0.5)
+        nc.scalar.activation(gn_half[:], gn_t[:], ACT.Copy, scale=half[:, 1:2])
 
-        y_ps = {}
-        xw_g = [sb("xw_g%d" % u, [P, HALF], U32) for u in range(2)]
+        xw_picked = [sb("xw_picked0", [P, HALF], U32), sb("xw_picked1", [P, HALF], U32, "w1s_raw")]
 
         def gather_words(u):
-            nc.vector.tensor_copy(xw_g[u][:], xw[:].bitcast(U32).indirect(offs_t[:, 16 * u : 16 * (u + 1)]))
+            nc.vector.tensor_copy(xw_picked[u][:], xw[:].bitcast(U32).indirect(entries(offs_t, u * HALF, HALF)))
 
+        w1w = sb("w1w", [P, H], I32)
+        w1s = sb("w1s", [P, H], U8)
         gather_words(0)
-        w1w = deal("w1w", w1w_raw, I32)
-        w1s = deal("w1s", w1s_raw, U8)
+        deal(w1w, w1w_raw, 0, 1)
+        deal(w1s, w1s_raw, 0, PACK)
         gather_words(1)
+        deal(w1w, w1w_raw, 1, PACK)
+
+        def product(out, words, scales, t, rhs_words, rhs_scales):
+            cols = slice(t * P, (t + 1) * P)
+            nc.tensor.matmul_mx(
+                out=out,
+                lhsT=words[:, cols].bitcast(FP8X4),
+                lhsT_scale=scales[:, cols],
+                rhs=rhs_words.bitcast(FP8X4),
+                rhs_scale=rhs_scales,
+                start=True,
+                stop=True,
+            )
+
+        halves = [slice(u * HALF, (u + 1) * HALF) for u in range(2)]
+        y_bank = {}
         for t in range(PACK):
             for u in range(2):
                 if u == 0 or t == 0:
-                    y_ps[t, u] = psum.tile([P, S], F32, name="acc", tag="acc")
+                    y_bank[t, u] = psum.tile([P, S], F32, name="acc", tag="acc")
                 else:
-                    y_ps[t, u] = y_ps[t, 0]
-                nc.tensor.matmul_mx(
-                    out=y_ps[t, u][:, u * HALF : (u + 1) * HALF],
-                    lhsT=w1w[:, t * P : (t + 1) * P].bitcast(FP8X4),
-                    lhsT_scale=w1s[W1_ROW:P, t * P : (t + 1) * P],
-                    rhs=xw_g[u][:].bitcast(FP8X4),
-                    rhs_scale=xs_g[:, u * HALF : (u + 1) * HALF],
-                    start=True,
-                    stop=True,
-                )
+                    y_bank[t, u] = y_bank[t, 0]
+                product(y_bank[t, u][:, halves[u]], w1w, w1s, t, xw_picked[u][:], xs_picked[:, halves[u]])
 
-        w2w = deal("w2w", w2w_raw, I32)
+        w2w = sb("w2w", [P, N], I32)
+        deal(w2w, w2w_raw, 0, PACK)
 
-        ya = [sb("ya%d" % t, [P, S], F32) for t in range(PACK)]
-        yb = [sb("yb%d" % t, [P, S], F32) for t in range(PACK)]
-        sc = [sb("sc%d" % t, [P, S], F32) for t in range(PACK)]
-        sh = [sb("sh%d" % t, [P, S], F32) for t in range(PACK)]
-
-        def evict(dst, t, u, cols):
-            nc.scalar.activation(dst[t][:, cols], y_ps[t, u][:, cols], ACT.Copy, scale=gn_half[:, t : t + 1])
+        y_tile = [sb("y_tile0", [P, S], F32)] + [sb("y_tile%d" % t, [P, 2 * S], F32) for t in range(1, PACK)]
+        y_window = [y_tile[t][:, 0:S] for t in range(PACK)]
+        y_plain = [y_tile[t + 1][:, S : 2 * S] for t in range(PACK - 1)] + [sb("y_plain_last", [P, S], F32)[:]]
+        c_tile = [sb("c_tile%d" % t, [P, S], F32) for t in range(PACK)]
+        minus_2c = [sb("minus_2c%d" % t, [P, S], F32) for t in range(PACK)]
 
         for t in range(PACK):
-            if t == 0:
-                for u in range(2):
-                    evict(ya, t, u, slice(u * HALF, (u + 1) * HALF))
-                    evict(yb, t, u, slice(u * HALF, (u + 1) * HALF))
-            else:
-                evict(ya, t, 0, slice(0, S))
-                evict(yb, t, 0, slice(0, S))
-            for u in range(2):
-                cols = slice(u * HALF, (u + 1) * HALF)
-                nc.vector.tensor_tensor(
-                    sc[t][:, cols], ya[t][:].indirect(n1_t[:, 16 * u : 16 * (u + 1)]), yb[t][:, cols], ALU.subtract
-                )
-        w2s = deal("w2s", w2s_raw, U8, "yb0")
+            pieces = halves if t == 0 else [slice(0, S)]
+            for u, cols in enumerate(pieces):
+                for dst in (y_window, y_plain):
+                    nc.scalar.activation(dst[t][:, cols], y_bank[t, u][:, cols], ACT.Copy, scale=gn_half[:, t : t + 1])
+            for cols in pieces:
+                looked_up = y_tile[t][:].indirect(entries(n1_t, cols.start, cols.stop - cols.start))
+                nc.vector.tensor_tensor(c_tile[t][:, cols], looked_up, y_plain[t][:, cols], ALU.subtract)
+        w2s = sb("w2s", [P, N], U8, "y_tile0")
+        deal(w2s, w2s_raw, 0, PACK)
         for t in range(PACK):
-            nc.scalar.activation(sh[t][:], sc[t][:], ACT.Copy, scale=-2.0)
+            nc.scalar.activation(minus_2c[t][:], c_tile[t][:], ACT.Copy, scale=-2.0)
 
-        ht = [sb("ht%d" % t, [P, S], F32) for t in range(PACK)]
-        shared = sb("shared", [P, 768], F32)
-        zb = [shared[:, 0:512].bitcast(BF16), shared[:, 512:768].bitcast(BF16), sb("zb2", [P, 512], BF16)[:]]
-        zfs = [sb("zf0", [P, 1024], F32)[:], sb("zf1", [P, 512], F32)[:], shared[:, 256:768]]
+        h_tile = [sb("h_tile%d" % t, [P, S], F32) for t in range(PACK)]
+        words0, words1, wide2 = PACK * CHUNKS[0][1] // 2, PACK * CHUNKS[1][1] // 2, PACK * CHUNKS[2][1]
+        shared = sb("shared", [P, words0 + words1], F32)
+        z_bf16 = [
+            shared[:, 0:words0].bitcast(BF16),
+            shared[:, words0 : words0 + words1].bitcast(BF16),
+            sb("z_bf16_last", [P, wide2], BF16)[:],
+        ]
+        z_f32 = [
+            sb("z_f32_0", [P, PACK * CHUNKS[0][1]], F32)[:],
+            sb("z_f32_1", [P, PACK * CHUNKS[1][1]], F32)[:],
+            shared[:, words0 + words1 - wide2 : words0 + words1],
+        ]
 
         def gather_z(c, tiles):
-            c0, w = CHUNKS[c]
+            start, width = CHUNKS[c]
             for t in tiles:
                 nc.vector.tensor_tensor(
-                    zfs[c][:, t * w : (t + 1) * w],
-                    sc[t][:].indirect(n1_t[:, c0 // 16 : (c0 + w) // 16]),
-                    sh[t][:, c0 : c0 + w],
+                    z_f32[c][:, t * width : (t + 1) * width],
+                    c_tile[t][:].indirect(entries(n1_t, start, width)),
+                    minus_2c[t][:, start : start + width],
                     ALU.add,
                 )
 
-        def weave(c):
-            dst = zb[c].rearrange("p (c i t) -> p c t i", i=4, t=PACK)
-            src = zfs[c].rearrange("p (t c i) -> p c t i", i=4, t=PACK)
-            if c == len(CHUNKS) - 1:
-                nc.vector.tensor_copy(out=dst, in_=src)
-            else:
-                nc.scalar.copy(out=dst, in_=src)
+        def weave(c, copy):
+            copy(
+                out=z_bf16[c].rearrange("p (a i t) -> p a t i", i=LINE, t=PACK),
+                in_=z_f32[c].rearrange("p (t a i) -> p a t i", i=LINE, t=PACK),
+            )
 
         def second_layer(c):
-            c0, w = CHUNKS[c]
-            zw = sb("zw%d" % c, [P, w], U32)
-            zs = sb("zs%d" % c, [P, w], U8)
-            nc.vector.quantize_mx(out=zw[:].bitcast(FP8X4), scales=zs[:], in_=zb[c])
+            start, width = CHUNKS[c]
+            zw = sb("zw%d" % c, [P, width], U32)
+            zs = sb("zs%d" % c, [P, width], U8)
+            nc.vector.quantize_mx(out=zw[:].bitcast(FP8X4), scales=zs[:], in_=z_bf16[c])
             for t in range(PACK):
                 acc = psum.tile([P, S], F32, name="acc", tag="acc")
-                nc.tensor.matmul_mx(
-                    out=acc[:, :w],
-                    lhsT=w2w[:, t * P : (t + 1) * P].bitcast(FP8X4),
-                    lhsT_scale=w2s[W2_ROW:P, t * P : (t + 1) * P],
-                    rhs=zw[:].bitcast(FP8X4),
-                    rhs_scale=zs[:],
-                    start=True,
-                    stop=True,
-                )
-                nc.scalar.copy(ht[t][:, c0 : c0 + w], acc[:, :w])
+                product(acc[:, :width], w2w, w2s, t, zw[:], zs[:])
+                nc.scalar.copy(h_tile[t][:, start : start + width], acc[:, :width])
 
         gather_z(0, range(PACK))
-        weave(0)
+        weave(0, nc.scalar.copy)
         gather_z(1, range(PACK))
-        weave(1)
+        weave(1, nc.scalar.copy)
         second_layer(0)
         gather_z(2, (0, 1))
         second_layer(1)
         gather_z(2, (2, 3))
-        weave(2)
+        weave(2, nc.vector.tensor_copy)
         second_layer(2)
 
         out_rows = out_0.rearrange("(p t) n -> t p n", t=PACK)
-        ob = sb("ob", [P, S, PACK], BF16)
+        out_bf16 = sb("out_bf16", [P, S, PACK], BF16)
         pa = [sb("pa%d" % t, [P, W], F32) for t in range(PACK)]
-        sg = [sb("sg%d" % t, [P, W], F32) for t in range(PACK)]
+        gate = [sb("gate%d" % t, [P, W], F32) for t in range(PACK)]
         for t in range(PACK):
-            nc.scalar.activation(sg[t][:], ht[t][:].indirect(n3_t[:]), ACT.Sigmoid)
-        nc.vector.tensor_copy(pa[0][:], ht[0][:].indirect(n2_t[:]))
+            nc.scalar.activation(gate[t][:], h_tile[t][:].indirect(n3_t[:]), ACT.Sigmoid)
+        last = PACK - 1
+        nc.vector.tensor_copy(pa[0][:], h_tile[0][:].indirect(n2_t[:]))
         for t in range(PACK):
-            if t + 1 < PACK:
-                nc.vector.tensor_copy(pa[t + 1][:], ht[t + 1][:].indirect(n2_t[:]))
-            if t == 3:
-                nc.vector.tensor_copy(ob[:, :V_COLS, 2], ht[2][:, :V_COLS])
-            nc.vector.tensor_tensor(ht[t][:].indirect(n3_t[:]), pa[t][:], sg[t][:], ALU.mult)
-            nc.sync.dma_start(out=out_rows[t], in_=ht[t][:])
-            if t < 2:
-                nc.scalar.copy(ob[:, :, t], ht[t][:])
+            if t < last:
+                nc.vector.tensor_copy(pa[t + 1][:], h_tile[t + 1][:].indirect(n2_t[:]))
             else:
-                nc.scalar.copy(ob[:, V_COLS:, t], ht[t][:, V_COLS:])
-        nc.vector.tensor_copy(ob[:, :V_COLS, 3], ht[3][:, :V_COLS])
+                nc.vector.tensor_copy(out_bf16[:, halves[0], last - 1], h_tile[last - 1][:, halves[0]])
+            nc.vector.tensor_tensor(h_tile[t][:].indirect(n3_t[:]), pa[t][:], gate[t][:], ALU.mult)
+            nc.sync.dma_start(out=out_rows[t], in_=h_tile[t][:])
+            cols = slice(0, S) if t < last - 1 else halves[1]
+            nc.scalar.copy(out_bf16[:, cols, t], h_tile[t][:, cols])
+        nc.vector.tensor_copy(out_bf16[:, halves[0], last], h_tile[last][:, halves[0]])
 
-        ow = sb("ow", [P, S], I32)
-        osc = sb("osc", [P, S], U8)
-        out_words = words_of(out_1)
-        for u in range(2):
-            cols = slice(u * HALF, (u + 1) * HALF)
+        out_w = sb("out_w", [P, S], I32)
+        out_s = sb("out_s", [P, S], U8)
+        for cols in halves:
             nc.vector.quantize_mx(
-                out=ow[:, cols].bitcast(FP8X4), scales=osc[:, cols], in_=ob[:, cols, :].rearrange("p n t -> p (n t)")
+                out=out_w[:, cols].bitcast(FP8X4),
+                scales=out_s[:, cols],
+                in_=out_bf16[:, cols, :].rearrange("p n t -> p (n t)"),
             )
-            nc.sync.dma_start(out=out_words[:, cols], in_=ow[:, cols])
-        for q in range(4):
-            nc.scalar.dma_start(
-                out=out_2[0, 4 * q : 4 * q + 4, :].bitcast(I32), in_=osc[32 * q : 32 * q + 4, :].bitcast(I32)
-            )
+            nc.sync.dma_start(out=words_of(out_1)[:, cols], in_=out_w[:, cols])
+        for q in range(P // QUADRANT):
+            nc.scalar.dma_start(out=scale_rows(out_2, q), in_=live_rows(out_s, q))

from contextlib import ExitStack

import concourse.mybir as mybir

K, T, S, N, H, W = 512, 2048, 512, 512, 512, 256
FLOPS = 2 * K * H * S + 2 * H * N * S

F32 = mybir.dt.float32
BF16 = mybir.dt.bfloat16
I32 = mybir.dt.int32
U32 = mybir.dt.uint32
U16 = mybir.dt.uint16
U8 = mybir.dt.uint8
FP8X4 = mybir.dt.float8_e4m3fn_x4
ALU = mybir.AluOpType
ACT = mybir.ActivationFunctionType

P = 128
PACK = 4
QUADRANT = 32
LIST_COL = 16
LINE = 4
HALF = S // 2
PSUM_BANKS = 8
CHUNKS = ((0, 256), (256, 128), (384, 128))


def tile_picked_laytwicefold_none_po_kernel(
    tc, x_words, x_scales, w1_words, w1_scales, gn, w2_words, w2_scales, offs, n1, n2, n3, out_0, out_1, out_2
):
    nc = tc.nc
    with ExitStack() as ctx:
        keep = ctx.enter_context(tc.tile_pool(name="keep", bufs=1))
        psum = ctx.enter_context(tc.psum_pool(name="psum", bufs=PSUM_BANKS))

        def sb(name, shape, dtype, tag=None):
            return keep.tile(shape, dtype, name=name, tag=tag or name, align_bytes=64)

        def words_of(dram):
            return dram[0].rearrange("p n r -> p (n r)").bitcast(I32)

        def entries(list_tile, start, count):
            return list_tile[:, start // LIST_COL : (start + count) // LIST_COL]

        def scale_rows(dram, q):
            return dram[0, PACK * q : PACK * (q + 1), :].bitcast(I32)

        def live_rows(tile, q):
            return tile[QUADRANT * q : QUADRANT * q + PACK, :].bitcast(I32)

        offs_t = keep.tile([P, S // LIST_COL], U16, name="offs_t")
        n1_t = keep.tile([P, S // LIST_COL], U16, name="n1_t")
        n2_t = keep.tile([P, W // LIST_COL], U16, name="n2_t")
        n3_t = keep.tile([P, W // LIST_COL], U16, name="n3_t")
        xw = sb("xw", [P, T], I32)
        xs = sb("xs", [P, T], U8)
        w1w_raw = sb("w1w_raw", [P, H], I32)
        w1s_raw = sb("w1s_raw", [P, H], U8)
        w2w_raw = sb("w2w_raw", [P, N], I32)
        w2s_raw = sb("w2s_raw", [P, N], U8)
        gn_t = sb("gn_t", [P, PACK], F32)

        nc.vector.memset(w1s_raw[:].bitcast(I32), 0)
        nc.vector.memset(w2s_raw[:].bitcast(I32), 0)
        for q in range(P // QUADRANT):
            nc.sync.dma_start(
                out=xs[QUADRANT * q : QUADRANT * (q + 1), :].bitcast(I32),
                in_=scale_rows(x_scales, q).unsqueeze(0).to_broadcast([QUADRANT // PACK, PACK, T // 4]),
            )
        nc.sync.dma_start(offs_t[:], offs)
        nc.sync.dma_start(out=xw[:], in_=words_of(x_words))
        nc.sync.dma_start(out=w1w_raw[:], in_=words_of(w1_words))
        for q in range(P // QUADRANT):
            nc.sync.dma_start(out=live_rows(w1s_raw, q), in_=scale_rows(w1_scales, q))
        nc.sync.dma_start(n1_t[:], n1)
        nc.sync.dma_start(out=w2w_raw[:], in_=words_of(w2_words))
        for q in range(P // QUADRANT):
            nc.sync.dma_start(out=live_rows(w2s_raw, q), in_=scale_rows(w2_scales, q))
        nc.sync.dma_start(n2_t[:], n2)
        nc.sync.dma_start(n3_t[:], n3)
        nc.gpsimd.dma_start(out=gn_t[:], in_=gn.rearrange("(p t) o -> p (t o)", t=PACK))

        half = sb("half", [P, 2], F32)
        nc.gpsimd.memset(half[:, 0:1], 0.0)
        nc.scalar.activation(half[:, 1:2], half[:, 0:1], ACT.Sigmoid)

        def deal(dealt, raw, t0, t1):
            nc.vector.tensor_copy(
                out=dealt[:].rearrange("p (t m) -> p m t", t=PACK)[:, :, t0:t1],
                in_=raw[:].rearrange("p (m t) -> p m t", t=PACK)[:, :, t0:t1],
            )

        xs_picked = sb("xs_picked", [P, S], U8)
        nc.vector.tensor_copy(xs_picked[:], xs[:].indirect(offs_t[:]))
        gn_half = sb("gn_half", [P, PACK], F32)
        nc.scalar.activation(gn_half[:], gn_t[:], ACT.Copy, scale=half[:, 1:2])

        xw_picked = [sb("xw_picked0", [P, HALF], U32), sb("xw_picked1", [P, HALF], U32, "w1s_raw")]

        def gather_words(u):
            nc.vector.tensor_copy(xw_picked[u][:], xw[:].bitcast(U32).indirect(entries(offs_t, u * HALF, HALF)))

        w1w = sb("w1w", [P, H], I32)
        w1s = sb("w1s", [P, H], U8)
        gather_words(0)
        deal(w1w, w1w_raw, 0, 1)
        deal(w1s, w1s_raw, 0, PACK)
        gather_words(1)
        deal(w1w, w1w_raw, 1, PACK)

        def product(out, words, scales, t, rhs_words, rhs_scales):
            cols = slice(t * P, (t + 1) * P)
            nc.tensor.matmul_mx(
                out=out,
                lhsT=words[:, cols].bitcast(FP8X4),
                lhsT_scale=scales[:, cols],
                rhs=rhs_words.bitcast(FP8X4),
                rhs_scale=rhs_scales,
                start=True,
                stop=True,
            )

        halves = [slice(u * HALF, (u + 1) * HALF) for u in range(2)]
        y_bank = {}
        for t in range(PACK):
            for u in range(2):
                if u == 0 or t == 0:
                    y_bank[t, u] = psum.tile([P, S], F32, name="acc", tag="acc")
                else:
                    y_bank[t, u] = y_bank[t, 0]
                product(y_bank[t, u][:, halves[u]], w1w, w1s, t, xw_picked[u][:], xs_picked[:, halves[u]])

        w2w = sb("w2w", [P, N], I32)
        deal(w2w, w2w_raw, 0, PACK)

        y_tile = [sb("y_tile0", [P, S], F32)] + [sb("y_tile%d" % t, [P, 2 * S], F32) for t in range(1, PACK)]
        y_window = [y_tile[t][:, 0:S] for t in range(PACK)]
        y_plain = [y_tile[t + 1][:, S : 2 * S] for t in range(PACK - 1)] + [sb("y_plain_last", [P, S], F32)[:]]
        c_tile = [sb("c_tile%d" % t, [P, S], F32) for t in range(PACK)]
        minus_2c = [sb("minus_2c%d" % t, [P, S], F32) for t in range(PACK)]

        for t in range(PACK):
            pieces = halves if t == 0 else [slice(0, S)]
            for u, cols in enumerate(pieces):
                for dst in (y_window, y_plain):
                    nc.scalar.activation(dst[t][:, cols], y_bank[t, u][:, cols], ACT.Copy, scale=gn_half[:, t : t + 1])
            for cols in pieces:
                looked_up = y_tile[t][:].indirect(entries(n1_t, cols.start, cols.stop - cols.start))
                nc.vector.tensor_tensor(c_tile[t][:, cols], looked_up, y_plain[t][:, cols], ALU.subtract)
        w2s = sb("w2s", [P, N], U8, "y_tile0")
        deal(w2s, w2s_raw, 0, PACK)
        for t in range(PACK):
            nc.scalar.activation(minus_2c[t][:], c_tile[t][:], ACT.Copy, scale=-2.0)

        h_tile = [sb("h_tile%d" % t, [P, S], F32) for t in range(PACK)]
        words0, words1, wide2 = PACK * CHUNKS[0][1] // 2, PACK * CHUNKS[1][1] // 2, PACK * CHUNKS[2][1]
        shared = sb("shared", [P, words0 + words1], F32)
        z_bf16 = [
            shared[:, 0:words0].bitcast(BF16),
            shared[:, words0 : words0 + words1].bitcast(BF16),
            sb("z_bf16_last", [P, wide2], BF16)[:],
        ]
        z_f32 = [
            sb("z_f32_0", [P, PACK * CHUNKS[0][1]], F32)[:],
            sb("z_f32_1", [P, PACK * CHUNKS[1][1]], F32)[:],
            shared[:, words0 + words1 - wide2 : words0 + words1],
        ]

        def gather_z(c, tiles):
            start, width = CHUNKS[c]
            for t in tiles:
                nc.vector.tensor_tensor(
                    z_f32[c][:, t * width : (t + 1) * width],
                    c_tile[t][:].indirect(entries(n1_t, start, width)),
                    minus_2c[t][:, start : start + width],
                    ALU.add,
                )

        def weave(c, copy):
            copy(
                out=z_bf16[c].rearrange("p (a i t) -> p a t i", i=LINE, t=PACK),
                in_=z_f32[c].rearrange("p (t a i) -> p a t i", i=LINE, t=PACK),
            )

        def second_layer(c):
            start, width = CHUNKS[c]
            zw = sb("zw%d" % c, [P, width], U32)
            zs = sb("zs%d" % c, [P, width], U8)
            nc.vector.quantize_mx(out=zw[:].bitcast(FP8X4), scales=zs[:], in_=z_bf16[c])
            for t in range(PACK):
                acc = psum.tile([P, S], F32, name="acc", tag="acc")
                product(acc[:, :width], w2w, w2s, t, zw[:], zs[:])
                nc.scalar.copy(h_tile[t][:, start : start + width], acc[:, :width])

        gather_z(0, range(PACK))
        weave(0, nc.scalar.copy)
        gather_z(1, range(PACK))
        weave(1, nc.scalar.copy)
        second_layer(0)
        gather_z(2, (0, 1))
        second_layer(1)
        gather_z(2, (2, 3))
        weave(2, nc.vector.tensor_copy)
        second_layer(2)

        out_rows = out_0.rearrange("(p t) n -> t p n", t=PACK)
        out_bf16 = sb("out_bf16", [P, S, PACK], BF16)
        pa = [sb("pa%d" % t, [P, W], F32) for t in range(PACK)]
        gate = [sb("gate%d" % t, [P, W], F32) for t in range(PACK)]
        for t in range(PACK):
            nc.scalar.activation(gate[t][:], h_tile[t][:].indirect(n3_t[:]), ACT.Sigmoid)
        last = PACK - 1
        nc.vector.tensor_copy(pa[0][:], h_tile[0][:].indirect(n2_t[:]))
        for t in range(PACK):
            if t < last:
                nc.vector.tensor_copy(pa[t + 1][:], h_tile[t + 1][:].indirect(n2_t[:]))
            else:
                nc.vector.tensor_copy(out_bf16[:, halves[0], last - 1], h_tile[last - 1][:, halves[0]])
            nc.vector.tensor_tensor(h_tile[t][:].indirect(n3_t[:]), pa[t][:], gate[t][:], ALU.mult)
            nc.sync.dma_start(out=out_rows[t], in_=h_tile[t][:])
            cols = slice(0, S) if t < last - 1 else halves[1]
            nc.scalar.copy(out_bf16[:, cols, t], h_tile[t][:, cols])
        nc.vector.tensor_copy(out_bf16[:, halves[0], last], h_tile[last][:, halves[0]])

        out_w = sb("out_w", [P, S], I32)
        out_s = sb("out_s", [P, S], U8)
        for cols in halves:
            nc.vector.quantize_mx(
                out=out_w[:, cols].bitcast(FP8X4),
                scales=out_s[:, cols],
                in_=out_bf16[:, cols, :].rearrange("p n t -> p (n t)"),
            )
            nc.sync.dma_start(out=words_of(out_1)[:, cols], in_=out_w[:, cols])
        for q in range(P // QUADRANT):
            nc.scalar.dma_start(out=scale_rows(out_2, q), in_=live_rows(out_s, q))
